import numpy as np
import ml_dtypes


def mxq(x, axis, fmt="e4m3"):
    dtype, down = {"e4m3": (ml_dtypes.float8_e4m3fn, 7), "e5m2": (ml_dtypes.float8_e5m2, 14)}[fmt]
    v = np.moveaxis(np.asarray(x, np.float32).astype(ml_dtypes.bfloat16).astype(np.float64), axis, -1)
    blocks = v.reshape(v.shape[:-1] + (-1, 32))
    amax = np.abs(blocks).max(-1, keepdims=True)
    byte = np.maximum(np.where(amax > 0, np.frexp(amax)[1] - 1 + 127, 0) - down, 1)
    scale = np.exp2(byte - 127.0)
    codes = (blocks / scale).astype(np.float32).astype(dtype).astype(np.float64)
    return np.moveaxis((codes * scale).reshape(v.shape), -1, axis)


WIDE = False


def mx_kscale(k):
    if not WIDE:
        return np.ones(k)
    levels = np.array([10, -10, 5, -5, 0])
    if k % 512:
        return np.exp2(np.random.permutation(np.resize(levels, k // 32))).repeat(32)
    a = np.empty((k // 512, 16))
    for p in range(k // 512):
        a[p, :8] = np.random.permutation(np.resize(levels, 8))
        for g in range(8):
            far = levels[np.abs(levels - a[p, g]) >= 10]
            a[p, g + 8] = far[np.random.randint(len(far))]
    return np.exp2(a.ravel()).repeat(32)


BF16 = ml_dtypes.bfloat16


def bf(x):
    return np.asarray(x, np.float32).astype(BF16)


def f64(x):
    return np.asarray(x).astype(np.float64)


E2M1 = np.array([0.0, 0.5, 1.0, 1.5, 2.0, 3.0, 4.0, 6.0, -0.0, -0.5, -1.0, -1.5, -2.0, -3.0, -4.0, -6.0])


def pack_weight(w, fmt):
    k, n = w.shape
    w = f64(bf(w)).reshape(k // 32, 32, n)
    amax = np.abs(w).max(1)
    if fmt == "e4m3":
        byte = np.frexp(amax)[1] - 1 + 127 - 7
    else:
        mant, ex = np.frexp(amax / 6.0)
        byte = np.where(mant > 0.5, ex, ex - 1) + 127
    byte = np.clip(np.where(amax > 0, byte, 1), 1, 254)
    scaled = (w * np.exp2(127.0 - byte)[:, None, :]).reshape(k, n).astype(np.float32)
    by_word = np.ascontiguousarray(scaled.reshape(k // 512, 128, 4, n).transpose(0, 1, 3, 2))
    if fmt == "e4m3":
        words = by_word.astype(ml_dtypes.float8_e4m3fn).view(np.uint8)
    else:
        c = by_word.astype(ml_dtypes.float4_e2m1fn).view(np.uint8) & 0xF
        words = c[..., 0::2] | (c[..., 1::2] << 4)
    return np.ascontiguousarray(words), np.ascontiguousarray(byte.astype(np.uint8).reshape(k // 512, 16, n))


def unpack_weight(words, scales, fmt):
    g, p, n, _ = words.shape
    if fmt == "e4m3":
        vals = np.ascontiguousarray(words).view(ml_dtypes.float8_e4m3fn).astype(np.float64)
    else:
        nib = np.empty((g, p, n, 4), np.uint8)
        nib[..., 0::2] = words & 0xF
        nib[..., 1::2] = words >> 4
        vals = E2M1[nib]
    vals = vals * np.repeat(np.exp2(scales.astype(np.float64) - 127.0), 8, axis=1)[..., None]
    return vals.transpose(0, 1, 3, 2).reshape(g * 512, n)

def planes(Y):
    n, m = Y.shape
    b = f64(bf(Y)).reshape(n // 32, 32, m)
    amax = np.abs(b).max(1)
    byte = np.clip(np.where(amax > 0, np.frexp(amax)[1] - 1 + 127 - 7, 1), 1, 254)
    codes = (b * np.exp2(127.0 - byte)[:, None, :]).reshape(n, m).astype(np.float32).astype(ml_dtypes.float8_e4m3fn).view(np.uint8)
    words = codes.reshape(n // 512, 128, 4, m).transpose(0, 1, 3, 2)
    return np.ascontiguousarray(words), np.ascontiguousarray(byte.astype(np.uint8).reshape(n // 512, 16, m))


B, Z, H, C, L, A = 1024, 512, 1024, 512, 64, 20
O = L * A


def sigmoid(v):
    return 1.0 / (1.0 + np.exp(-v))


def _gated_output_weight(w, s, dictionary):
    ws = w * sigmoid(s)
    return mxq(ws, 1, "e4m3") @ dictionary


def _log_normalize(logits):
    m = logits.max(-1, keepdims=True)
    return logits - (m + np.log(np.sum(np.exp(logits - m), axis=-1, keepdims=True)))


def setup_inputs():
    p, t, u = mx_kscale(Z), mx_kscale(H), mx_kscale(C)
    z = bf(np.random.standard_normal((B, Z)) * p)
    w1_words, w1_scales = pack_weight(np.random.standard_normal((Z, H)) / np.sqrt(Z) / p[:, None] * t, "e4m3")
    b1 = bf(np.random.standard_normal(H) * 0.3 * t)
    w = bf(np.random.standard_normal((H, C)) * 4.0 / np.sqrt(H) / t[:, None] * u)
    s = bf(np.random.standard_normal((H, C)))
    dict_words, dict_scales = pack_weight(np.random.standard_normal((C, O)) / np.sqrt(C) / u[:, None], "e4m3")
    b = bf(np.random.standard_normal(O) * 0.5)
    return {
        "z": z,
        "w1_words": w1_words,
        "w1_scales": w1_scales,
        "b1": b1,
        "w": w,
        "s": s,
        "dict_words": dict_words,
        "dict_scales": dict_scales,
        "b": b,
    }


def core(z, w1_words, w1_scales, b1, w, s, dict_words, dict_scales, b):
    h = np.maximum((mxq(f64(z), 1, "e4m3") @ unpack_weight(w1_words, w1_scales, "e4m3")) + f64(b1), 0.0)
    weff = _gated_output_weight(f64(w), f64(s), unpack_weight(dict_words, dict_scales, "e4m3"))
    logits = (mxq(h, 1, "e4m3") @ mxq(weff, 0, "e4m3")) + f64(b)
    logits = np.reshape(logits, (z.shape[0], L, A))
    return _log_normalize(logits)


def reference(z, w1_words, w1_scales, b1, w, s, dict_words, dict_scales, b):
    R_out = core(z, w1_words, w1_scales, b1, w, s, dict_words, dict_scales, b)
    words, scales = planes(np.moveaxis(R_out, 0, 0).reshape(1024, -1))
    return R_out, words, scales

from contextlib import ExitStack

import concourse.mybir as mybir
from concourse.masks import make_identity

ACT = mybir.ActivationFunctionType
ALU = mybir.AluOpType
AX = mybir.AxisListType
F32 = mybir.dt.float32
BF16 = mybir.dt.bfloat16
I32 = mybir.dt.int32
U8 = mybir.dt.uint8
FP8X4 = mybir.dt.float8_e4m3fn_x4

B, Z, H, C, L, A = 1024, 512, 1024, 512, 64, 20
O = L * A
P = 128
HALF = O // 2
LH = L // 2
PLAN = """
SG.0.s GM.0.v.0 GM.0.g.1 SG.1.s GM.1.g.0 GM.1.v.1 BM.0.p BC.0.v BM.1.p BC.1.s BM.2.p BC.2.v W1.1.v TZ.0.p
CZ.0.v TZ.1.p CZ.1.v W1.0.v QZ.0.v TW.0.p CW.0.v TW.1.p CW.1.v SG.2.s GM.2.g.0 GM.2.g.1 SG.3.s GM.3.g.0
GM.3.v.1 QW.0.v HM.0.p.0 HR.0.s.0 HM.0.p.1 HR.0.s.1 HM.0.p.2 HR.0.s.2 HM.0.p.3 HR.0.s.3 HL.0.v QH.0.v TW.2.p
CW.2.v TW.3.p CW.3.v QW.1.v EM.0.p EC.0.s EM.1.p EC.1.s EM.2.p EC.2.s EM.3.p EC.3.s EM.4.p EC.4.s HM.1.p.0
HR.1.s.0 HM.1.p.1 HR.1.s.1 HM.1.p.2 HR.1.s.2 HM.1.p.3 HR.1.s.3 HL.1.v QH.1.v QE.0.v.0 QE.0.v.1 EM.5.p EC.5.s
EM.6.p EC.6.s EM.7.p EC.7.s EM.8.p EC.8.s EM.9.p EC.9.s QE.1.v.0 QE.1.v.1 TZ.2.p CZ.2.s TZ.3.p CZ.3.s QZ.1.v
MM.0.p.0.0 MM.0.p.1.0 MM.0.p.0.1 MM.0.p.1.1 AD.0.v.0 AD.0.v.1 MM.1.p.0.0 MM.1.p.1.0 MM.1.p.0.1 MM.1.p.1.1
AD.1.v.0 AD.1.v.1 MX.0.v SU.0.g EU.0.s HM.2.p.0 HR.2.s.0 HM.2.p.1 HR.2.s.1 HM.2.p.2 HR.2.s.2 HM.2.p.3 HR.2.s.3
HL.2.v QH.2.v HM.3.p.0 HR.3.s.0 HM.3.p.1 HR.3.s.1 HM.3.p.2 HR.3.s.2 HM.3.p.3 HR.3.s.3 HL.3.v QH.3.v MM.2.p.0.0
MM.2.p.1.0 MM.2.p.0.1 MM.2.p.1.1 AD.2.v.0 AD.2.v.1 MX.1.v SU.1.g EU.1.s MM.3.p.0.0 MM.3.p.1.0 MM.3.p.0.1
MM.3.p.1.1 AD.3.v.0 AD.3.v.1 MX.2.v SU.2.g EU.2.s EM.10.p EC.10.s EM.11.p EC.11.s EM.12.p EC.12.s EM.13.p
EC.13.s EM.14.p EC.14.s QE.2.v.0 QE.2.v.1 MM.4.p.0.0 MM.4.p.1.0 MM.4.p.0.1 MM.4.p.1.1 AD.4.v.0 AD.4.v.1 MX.3.v
SU.3.g EU.3.s EM.15.p EC.15.s EM.16.p EC.16.s EM.17.p EC.17.s EM.18.p EC.18.s EM.19.p EC.19.s QE.3.v.0
QE.3.v.1 MM.5.p.0.0 MM.5.p.1.0 MM.5.p.0.1 MM.5.p.1.1 AD.5.v.0 AD.5.v.1 MX.4.v SU.4.g EU.4.s MM.6.p.0.0
MM.6.p.1.0 MM.6.p.0.1 MM.6.p.1.1 AD.6.v.0 AD.6.v.1 MX.5.v SU.5.g EU.5.s MM.7.p.0.0 MM.7.p.1.0 MM.7.p.0.1
MM.7.p.1.1 AD.7.v.0 AD.7.v.1 MX.6.v SU.6.g EU.6.s MM.8.p.0.0 MM.8.p.1.0 MM.8.p.0.1 MM.8.p.1.1 AD.8.v.0
AD.8.v.1 MX.7.v SU.7.g EU.7.s EG.0.p.0 EG.0.p.1 MM.9.p.0.0 MM.9.p.1.0 MM.9.p.0.1 MM.9.p.1.1 AD.9.v.0 AD.9.v.1
MX.8.v SU.8.g EU.8.s EG.0.p.2 EG.0.p.3 MM.10.p.0.0 MM.10.p.1.0 MM.10.p.0.1 MM.10.p.1.1 AD.10.v.0 AD.10.v.1
MX.9.v SU.9.g EU.9.s EG.0.p.4 MM.11.p.0.0 MM.11.p.1.0 MM.11.p.0.1 MM.11.p.1.1 AD.11.v.0 AD.11.v.1 MX.10.v
SU.10.g EU.10.s MM.12.p.0.0 MM.12.p.1.0 MM.12.p.0.1 MM.12.p.1.1 AD.12.v.0 AD.12.v.1 MX.11.v SU.11.g EU.11.s
LN.0.s LT.0.p KB.0.v EG.1.p.0 EG.1.p.1 MM.13.p.0.0 MM.13.p.1.0 MM.13.p.0.1 MM.13.p.1.1 AD.13.v.0 AD.13.v.1
MX.12.v SU.12.g EU.12.s EG.1.p.2 EG.1.p.3 MM.14.p.0.0 MM.14.p.1.0 MM.14.p.0.1 MM.14.p.1.1 AD.14.v.0 AD.14.v.1
MX.13.v SU.13.g EU.13.s EG.1.p.4 MM.15.p.0.0 MM.15.p.1.0 MM.15.p.0.1 MM.15.p.1.1 AD.15.v.0 AD.15.v.1 MX.14.v
SU.14.g EU.14.s MX.15.v SU.15.g EU.15.s EG.2.p.0 EG.2.p.1 EG.2.p.2 EG.2.p.3 EG.2.p.4 EG.3.p.0 EG.3.p.1
EG.3.p.2 EG.3.p.3 EG.3.p.4 LN.1.s LT.1.p KB.1.v LN.2.s LT.2.p KB.2.v LN.3.s LT.3.p KB.3.v FO.0.g FO.1.v FO.2.v
FO.3.v KA.0.g.0 KA.0.s.1 KA.0.v.2 KA.0.s.3 KA.0.v.4 QO.0.v.0 QO.0.v.1 FO.4.g FO.5.v FO.6.v FO.7.v KA.1.g.0
KA.1.s.1 KA.1.v.2 KA.1.s.3 KA.1.v.4 QO.1.v.0 QO.1.v.1 FO.8.g FO.9.v FO.10.v FO.11.v KA.2.v.0 KA.2.s.1 KA.2.v.2
KA.2.s.3 KA.2.v.4 QO.2.v.0 QO.2.v.1 FO.12.g FO.13.v FO.14.v FO.15.v KA.3.v.0 KA.3.s.1 KA.3.v.2 KA.3.s.3
KA.3.g.4 QO.3.v.0 QO.3.v.1
"""
FLOPS = 2 * B * Z * H + 2 * H * C * O + 2 * B * H * O


def tile_gateddictionaryproteinprofiledecoder_x2_kernel(
    tc, z, w1_words, w1_scales, b1, w, s, dict_words, dict_scales, b, out_0, out_1, out_2
):
    nc = tc.nc
    with ExitStack() as ctx:
        keep = ctx.enter_context(tc.tile_pool(name="keep", bufs=1))
        work = ctx.enter_context(tc.tile_pool(name="work", bufs=3))
        psum = ctx.enter_context(tc.psum_pool(name="psum", bufs=6))

        ident = keep.tile([P, P], F32, name="ident", align_bytes=64)
        ones = keep.tile([P, P], BF16, name="ones", align_bytes=64)
        brow = keep.tile([P, O], BF16, name="brow", align_bytes=64)
        b_all = keep.tile([P, O], BF16, name="b_all", align_bytes=64)
        b1_sb = keep.tile([P, 2, 4], BF16, name="b1_sb", align_bytes=64)
        tiny = keep.tile([P, 1], F32, name="tiny")
        tiny2 = keep.tile([P, 1], F32, name="tiny2")
        s_all = work.tile([P, 4, 2, C], BF16, name="s_all", tag="o", bufs=4, align_bytes=64)
        w_all = work.tile([P, 4, 2, C], BF16, name="w_all", tag="o", bufs=4, align_bytes=64)
        z_all = work.tile([P, 4, 2, Z], BF16, name="z_all", tag="o", bufs=4, align_bytes=64)
        s_sb, w_sb, z_sb = ([x[:, k] for k in range(4)] for x in (s_all, w_all, z_all))
        w1_raw = keep.tile([P, H], I32, name="w1_raw", align_bytes=64)
        w1_code = keep.tile([P, H], I32, name="w1_code", align_bytes=64)
        w1s_raw = keep.tile([P, H], U8, name="w1s_raw", align_bytes=64)
        w1_scale = keep.tile([P, H], U8, name="w1_scale", align_bytes=64)
        d_code = keep.tile([P, O], I32, name="d_code", align_bytes=64)
        d_scale = keep.tile([P, O], U8, name="d_scale", align_bytes=64)
        z_code = [keep.tile([P, 512], I32, name=f"z_code{g}", align_bytes=64) for g in range(2)]
        z_scale = [keep.tile([P, 512], U8, name=f"z_scale{g}", align_bytes=64) for g in range(2)]
        ws_code = [keep.tile([P, 512], I32, name=f"ws_code{g}", align_bytes=64) for g in range(2)]
        ws_scale = [keep.tile([P, 512], U8, name=f"ws_scale{g}", align_bytes=64) for g in range(2)]
        h_code = [[keep.tile([P, 512], I32, name=f"h_code{g}{k}", align_bytes=64) for k in range(2)] for g in range(2)]
        h_scale = [[keep.tile([P, 512], U8, name=f"h_scale{g}{k}", align_bytes=64) for k in range(2)] for g in range(2)]
        we_code = [[keep.tile([P, HALF], I32, name=f"we_code{g}{k}", align_bytes=64) for k in range(2)] for g in range(2)]
        we_scale = [[keep.tile([P, HALF], U8, name=f"we_scale{g}{k}", align_bytes=64) for k in range(2)] for g in range(2)]
        planes = [keep.tile([P, O], U8, name=f"plane{g}", align_bytes=64) for g in range(2)]

        make_identity(nc, ident[:])
        nc.vector.memset(brow[:], 0.0)
        nc.vector.memset(tiny[:], 0.0)
        nc.vector.memset(w1s_raw[:].bitcast(I32), 0)
        nc.vector.memset(d_scale[:].bitcast(I32), 0)
        nc.vector.memset(ones[:], 1.0)
        nc.scalar.activation(tiny2[:], tiny[:], ACT.Sigmoid)

        def load(dst, src, k):
            g, a = divmod(k, 2)
            part = src[512 * g : 512 * g + 512, :].rearrange("(p t) c -> p t c", t=4)[:, 2 * a : 2 * a + 2, :]
            nc.sync.dma_start(out=dst[k][:], in_=part)

        w1_view = w1_words[0].rearrange("p n t -> p (n t)")
        d_view = dict_words[0].rearrange("p n t -> p (n t)")
        for Q in range(4):
            nc.gpsimd.dma_start(out=w1s_raw[32 * Q : 32 * Q + 4, :].bitcast(I32), in_=w1_scales[0, 4 * Q : 4 * Q + 4, :].bitcast(I32))
        load(s_sb, s, 0)
        load(s_sb, s, 1)
        nc.sync.dma_start(out=brow[0:1, :], in_=b.rearrange("(x n) -> x n", x=1))
        load(w_sb, w, 0)
        load(w_sb, w, 1)
        load(z_sb, z, 0)
        load(z_sb, z, 1)
        nc.sync.dma_start(out=b1_sb[:], in_=b1.rearrange("(g p t) -> p g t", g=2, t=4))
        nc.sync.dma_start(out=w1_raw[:], in_=w1_view.bitcast(I32))
        load(s_sb, s, 2)
        load(s_sb, s, 3)
        for Q in range(4):
            nc.sync.dma_start(out=d_scale[32 * Q : 32 * Q + 4, :].bitcast(I32), in_=dict_scales[0, 4 * Q : 4 * Q + 4, :].bitcast(I32))
        load(w_sb, w, 2)
        load(w_sb, w, 3)
        nc.sync.dma_start(out=d_code[:, 0:HALF], in_=d_view[:, 0 : 4 * HALF].bitcast(I32))
        load(z_sb, z, 2)
        load(z_sb, z, 3)
        nc.sync.dma_start(out=d_code[:, HALF:O], in_=d_view[:, 4 * HALF : 4 * O].bitcast(I32))

        def bank_tile(shape):
            return psum.tile(shape, F32, name="pb", tag="pb", bufs=7)

        def four():
            return work.tile([P, 512, 4], BF16, name="g4", tag="g4", bufs=4, align_bytes=64)

        def wide():
            return work.tile([P, HALF, 4], BF16, name="og", tag="og", bufs=4, align_bytes=64)

        def copy(eng, dst, src):
            if eng == "v":
                nc.vector.tensor_copy(dst, src)
            elif eng == "s":
                nc.scalar.copy(dst, src)
            else:
                nc.gpsimd.tensor_scalar(dst, src, 1.0, 0.0, ALU.mult, ALU.add)

        def quant_part(code, scale, src, at, wd):
            nc.vector.quantize_mx(
                out=code[:, at : at + wd].bitcast(FP8X4),
                scales=scale[:, at : at + wd],
                in_=src[:, at : at + wd, :].rearrange("p n t -> p (n t)"),
            )

        def by_letter(ap):
            return ap.rearrange("p (l a) -> p l a", a=A)

        def bcast(ap):
            return ap.unsqueeze(2).to_broadcast([P, LH, A])

        st = {}
        sums_all = psum.tile([P, 4, P], F32, name="sums_all", tag="sums_all", bufs=1)
        units = [(half, g, t) for half in range(2) for g in range(2) for t in range(4)]

        def lazy(key, make):
            if key not in st:
                st[key] = make()
            return st[key]

        def SG(k, e):
            sg = work.tile([P, 2, C], F32, name="sg", tag="sg", bufs=3)
            nc.scalar.activation(sg[:], s_sb[k][:], ACT.Sigmoid)
            st["sg", k] = sg

        def GM(k, e, t):
            sg = st["sg", k]
            st["gm", k, t] = 1
            (nc.gpsimd if e == "g" else nc.vector).tensor_tensor(w_sb[k][:, t, :], w_sb[k][:, t, :], sg[:, t, :], ALU.mult)

        def BM(i, e):
            c0, wd = ((0, 512), (512, 512), (1024, 256))[i]
            bank = bank_tile([P, 512])
            nc.tensor.matmul(bank[:, 0:wd], lhsT=ones[:], rhs=brow[:, c0 : c0 + wd], start=True, stop=True)
            st["bm", i] = bank

        def BC(i, e):
            c0, wd = ((0, 512), (512, 512), (1024, 256))[i]
            copy(e, b_all[:, c0 : c0 + wd], st["bm", i][:, 0:wd])

        def W1(i, e):
            dst, src = ((w1_code, w1_raw), (w1_scale, w1s_raw))[i]
            eng = nc.gpsimd if e == "g" else nc.vector
            eng.tensor_copy(dst[:].rearrange("p (g t m) -> p g t m", g=2, t=4), src[:].rearrange("p (g m t) -> p g t m", g=2, t=4))

        def turn(name, src, k):
            bank = bank_tile([P, 2, 256])
            words = src[k][:].rearrange("p t c -> p (t c)").bitcast(F32)
            for tt in range(2):
                for u in range(2):
                    nc.tensor.transpose(bank[:, u, 128 * tt : 128 * tt + 128], words[:, 256 * tt + u : 256 * tt + 256 : 2], ident[:])
            st[name, k] = bank

        def TZ(k, e):
            turn("tz", z_sb, k)

        def TW(k, e):
            assert ("gm", k, 0) in st and ("gm", k, 1) in st
            turn("tw", w_sb, k)

        def words_out(e, bank, dst, k):
            a = k % 2
            out = dst[:, 256 * a : 256 * a + 256, :].rearrange("p n t -> p (n t)").bitcast(F32).rearrange("p (n u) -> p n u", u=2)
            copy(e, out, bank[:].rearrange("p u n -> p n u"))

        def CZ(k, e):
            words_out(e, st["tz", k], lazy(("zg", k // 2), four), k)

        def CW(k, e):
            words_out(e, st["tw", k], lazy(("wsg", k // 2), four), k)

        def QZ(g, e):
            quant_part(z_code[g], z_scale[g], st["zg", g], 0, 512)

        def QW(g, e):
            quant_part(ws_code[g], ws_scale[g], st["wsg", g], 0, 512)

        def HM(b, e, t):
            gb, gh = divmod(b, 2)
            bank = bank_tile([P, 512])
            cols = slice(512 * gh + 128 * t, 512 * gh + 128 * t + 128)
            nc.tensor.matmul_mx(
                out=bank[:], lhsT=w1_code[:, cols].bitcast(FP8X4), lhsT_scale=w1_scale[:, cols],
                rhs=z_code[gb][:].bitcast(FP8X4), rhs_scale=z_scale[gb][:], start=True, stop=True,
            )
            st["hm", b, t] = bank

        def HR(b, e, t):
            gb, gh = divmod(b, 2)
            ht = lazy(("ht", b), lambda: work.tile([P, 4, 512], BF16, name="ht", tag="ht", bufs=2, align_bytes=64))
            if e == "v":
                nc.vector.tensor_scalar(ht[:, t, :], st["hm", b, t][:], b1_sb[:, gh, t : t + 1], 0.0, ALU.add, ALU.max)
            else:
                nc.scalar.activation(ht[:, t, :], st["hm", b, t][:], ACT.Relu, bias=b1_sb[:, gh, t : t + 1])

        def HL(b, e):
            hg = st["hg", b] = four()
            copy(e, hg[:].rearrange("p (c i) t -> p c t i", i=4), st["ht", b][:].rearrange("p t (c i) -> p c t i", i=4))

        def QH(b, e):
            gb, gh = divmod(b, 2)
            quant_part(h_code[gb][gh], h_scale[gb][gh], st["hg", b], 0, 512)

        def JM(b, e, j):
            gb, gh = divmod(b, 2)
            bank = st["jm", b, j] = bank_tile([P, 4, 128])
            for t in range(4):
                cols = slice(512 * gh + 128 * t, 512 * gh + 128 * t + 128)
                nc.tensor.matmul_mx(
                    out=bank[:, t, :], lhsT=w1_code[:, cols].bitcast(FP8X4), lhsT_scale=w1_scale[:, cols],
                    rhs=z_code[gb][:, 128 * j : 128 * j + 128].bitcast(FP8X4), rhs_scale=z_scale[gb][:, 128 * j : 128 * j + 128],
                    start=True, stop=True,
                )

        def JA(b, e, j):
            gh = b % 2
            hp = lazy(("hp", b), four)
            bias = b1_sb[:, gh, :].unsqueeze(1).to_broadcast([P, 128, 4])
            st["ja", b, j] = 1
            nc.vector.tensor_tensor(hp[:, 128 * j : 128 * j + 128, :], st["jm", b, j][:].rearrange("p t n -> p n t"), bias, ALU.add)

        def JR(b, e):
            assert all(("ja", b, j) in st for j in range(4))
            hg = st["hg", b] = st["hp", b]
            (nc.vector if e == "v" else nc.gpsimd).tensor_scalar(hg[:], hg[:], 0.0, 1.0, ALU.max, ALU.mult)

        def EM(x, e):
            hh, i = divmod(x, 5)
            half, gh = divmod(hh, 2)
            oc = 5 * half + i
            bank = bank_tile([P, 4, 128])
            for t in range(4):
                nc.tensor.matmul_mx(
                    out=bank[:, t, :],
                    lhsT=ws_code[gh][:, 128 * t : 128 * t + 128].bitcast(FP8X4),
                    lhsT_scale=ws_scale[gh][:, 128 * t : 128 * t + 128],
                    rhs=d_code[:, 128 * oc : 128 * oc + 128].bitcast(FP8X4),
                    rhs_scale=d_scale[:, 128 * oc : 128 * oc + 128],
                    start=True, stop=True,
                )
            st["em", x] = bank

        def EC(x, e):
            hh, i = divmod(x, 5)
            dst = lazy(("we", hh), wide)
            copy(e, dst[:, 128 * i : 128 * i + 128, :], st["em", x][:].rearrange("p t n -> p n t"))

        def QE(hh, e, part):
            half, gh = divmod(hh, 2)
            at, wd = ((0, 512), (512, 128))[part]
            quant_part(we_code[gh][half], we_scale[gh][half], st["we", hh], at, wd)

        def MM(u, e, gh, which):
            half, g, t = units[u]
            if gh == 0:
                st["mm", u, which] = bank_tile([P, 512])
            for bank, c0, wd in [(st["mm", u, which],) + ((0, 512), (512, 128))[which]]:
                nc.tensor.matmul_mx(
                    out=bank[:, 0:wd],
                    lhsT=h_code[g][gh][:, 128 * t : 128 * t + 128].bitcast(FP8X4),
                    lhsT_scale=h_scale[g][gh][:, 128 * t : 128 * t + 128],
                    rhs=we_code[gh][half][:, c0 : c0 + wd].bitcast(FP8X4),
                    rhs_scale=we_scale[gh][half][:, c0 : c0 + wd],
                    start=(gh == 0), stop=(gh == 1),
                )
            if gh == 1:
                st["m2", u, which] = st["mm", u, which]

        def AD(u, e, which):
            half, g, t = units[u]
            y = lazy(("y", u // 4), lambda: work.tile([P, 4, HALF], F32, name="y", tag="y", bufs=4))
            st["ad", u, which] = 1
            bank, c0, wd = (st["m2", u, which],) + ((0, 512), (512, 128))[which]
            nc.vector.tensor_tensor(y[:, t, c0 : c0 + wd], bank[:, 0:wd], b_all[:, half * HALF + c0 : half * HALF + c0 + wd], ALU.add)

        def MX(u, e):
            assert ("ad", u, 0) in st and ("ad", u, 1) in st
            q, t = divmod(u, 4)
            nm = lazy(("nm", q), lambda: work.tile([P, P], F32, name="nm", tag="nm", bufs=4))
            st["mx", u] = 1
            nc.vector.tensor_reduce(nm[:, LH * t : LH * t + LH], by_letter(st["y", q][:, t, :]), AX.X, ALU.max, negate=True)

        def TY(q, e, j):
            assert all(("mx", 4 * q + t) in st for t in range(4))
            bank = st["ty", q, j] = bank_tile([P, 4, P])
            yy = st["y", q][:].rearrange("p t (l a) -> p (t l) a", a=A)
            for i in range(4):
                nc.tensor.matmul(bank[:, i, :], lhsT=yy[:, :, 4 * j + i], rhs=ident[:], is_transpose=True, start=True, stop=False)
                nc.tensor.matmul(bank[:, i, :], lhsT=st["nm", q][:], rhs=ident[:], is_transpose=True, start=False, stop=True)

        def EX(q, e, j):
            ee = lazy(("e", q), lambda: work.tile([P, A, P], F32, name="e", tag="e", bufs=2))
            st["ex", q, j] = 1
            nc.scalar.activation(ee[:, 4 * j : 4 * j + 4, :], st["ty", q, j][:], ACT.Exp)

        def ES(q, e, j):
            assert st.get("es", 0) == j and ("ex", q, j) in st
            assert j == 0 or st["esq"] == q
            st["es"], st["esq"] = (j + 1) % 5, q
            for a in range(4 * j, 4 * j + 4):
                nc.tensor.matmul(sums_all[:, q, :], lhsT=st["e", q][:, a, :], rhs=ident[:], is_transpose=True, start=(a == 0), stop=(a == A - 1))
            if j == 4:
                st["sums", q] = sums_all[:, q, :]

        def SU(u, e):
            q, t = divmod(u, 4)
            assert ("mx", u) in st
            d = st["d", u] = work.tile([P, HALF], F32, name="d", tag="d", bufs=3)
            (nc.vector if e == "v" else nc.gpsimd).tensor_tensor(
                by_letter(d[:]), by_letter(st["y", q][:, t, :]), bcast(st["nm", q][:, LH * t : LH * t + LH]), ALU.add
            )

        def EU(u, e):
            q, t = divmod(u, 4)
            ee = lazy(("e", q), lambda: work.tile([P, 4, HALF], F32, name="e", tag="e", bufs=2))
            st["eu", u] = 1
            nc.scalar.activation(ee[:, t, :], st["d", u][:], ACT.Exp)

        def EG(q, e, j):
            assert st.get("es", 0) == j and all(("eu", 4 * q + t) in st for t in range(4))
            assert j == 0 or st["esq"] == q
            st["es"], st["esq"] = (j + 1) % 5, q
            ee = st["e", q][:].rearrange("p t (l a) -> p (t l) a", a=A)
            for a in range(4 * j, 4 * j + 4):
                nc.tensor.matmul(sums_all[:, q, :], lhsT=ee[:, :, a], rhs=ident[:], is_transpose=True, start=(a == 0), stop=(a == A - 1))
            if j == 4:
                st["sums", q] = sums_all[:, q, :]

        def LT(q, e):
            bank = st["back", q] = bank_tile([P, P])
            nc.tensor.transpose(bank[:], st["ln", q][:], ident[:])

        def KB(q, e):
            kk = st["kk", q] = work.tile([P, P], F32, name="kk", tag="kk", bufs=2)
            nc.vector.tensor_tensor(kk[:], st["nm", q][:], st["back", q][:], ALU.subtract)

        def LN(q, e):
            ln = st["ln", q] = work.tile([P, P], F32, name="ln", tag="ln", bufs=2)
            nc.scalar.activation(ln[:], st["sums", q], ACT.Ln)

        def KK(q, e):
            kk = st["kk", q] = work.tile([P, P], F32, name="kk", tag="kk", bufs=2)
            (nc.vector if e == "v" else nc.gpsimd).tensor_tensor(kk[:], st["nm", q][:], st["ln", q][:], ALU.subtract)

        def FO(u, e):
            half, g, t = units[u]
            q = u // 4
            o = lazy(("o", q), lambda: work.tile([P, 4, HALF], F32, name="o", tag="o", bufs=4, align_bytes=64))
            st["fo", u] = 1
            (nc.vector if e == "v" else nc.gpsimd).tensor_tensor(
                by_letter(o[:, t, :]), by_letter(st["y", q][:, t, :]), bcast(st["kk", q][:, LH * t : LH * t + LH]), ALU.add
            )
            out_rows = out_0[512 * g : 512 * g + 512].rearrange("(p t) l a -> p t (l a)", t=4)
            nc.sync.dma_start(out=out_rows[:, t, half * HALF : half * HALF + HALF], in_=o[:, t, :])

        def KA(q, e, i):
            assert all(("fo", 4 * q + t) in st for t in range(4))
            og = lazy(("og", q), wide)
            sl = slice(128 * i, 128 * i + 128)
            copy(e, og[:, sl, :], st["o", q][:, :, sl].rearrange("p t n -> p n t"))

        def QO(q, e, part):
            half, g, t = units[4 * q]
            oc = lazy(("oc", q), lambda: work.tile([P, HALF], I32, name="oc", tag="oc", bufs=2, align_bytes=64))
            cols = slice(half * HALF, half * HALF + HALF)
            at, wd = ((0, 512), (512, 128))[part]
            quant_part(oc, planes[g][:, cols], st["og", q], at, wd)
            st["qo", q, part] = 1
            if ("qo", q, 1 - part) in st:
                nc.sync.dma_start(out=out_1[g].rearrange("p m t -> p (m t)")[:, half * 4 * HALF : (half + 1) * 4 * HALF].bitcast(I32), in_=oc[:])
                for Q in range(4):
                    nc.sync.dma_start(out=out_2[g, 4 * Q : 4 * Q + 4, cols].bitcast(I32), in_=planes[g][32 * Q : 32 * Q + 4, cols].bitcast(I32))

        def TB(k, e):
            nc.scalar.activation(tiny2[:], tiny[:], (ACT.Exp, ACT.Ln)[k])

        do = dict(SG=SG, GM=GM, BM=BM, BC=BC, W1=W1, TZ=TZ, TW=TW, CZ=CZ, CW=CW, QZ=QZ, QW=QW, HM=HM, HR=HR, HL=HL, QH=QH, JM=JM, JA=JA, JR=JR, EM=EM, EC=EC,
                  QE=QE, MM=MM, AD=AD, MX=MX, EX=EX, ES=ES, LN=LN, KK=KK, KB=KB, LT=LT, EG=EG, EU=EU, SU=SU, TY=TY, FO=FO, KA=KA, QO=QO, TB=TB)
        for tok in PLAN.split():
            parts = tok.split(".")
            args = [int(x) for x in parts[3:]]
            do[parts[0]](int(parts[1]), parts[2], *args)
